import numpy as np
import ml_dtypes


def mxq(x, axis, fmt="e4m3"):
    dtype, down = {"e4m3": (ml_dtypes.float8_e4m3fn, 7), "e5m2": (ml_dtypes.float8_e5m2, 14)}[fmt]
    v = np.moveaxis(np.asarray(x, np.float32).astype(ml_dtypes.bfloat16).astype(np.float64), axis, -1)
    blocks = v.reshape(v.shape[:-1] + (-1, 32))
    amax = np.abs(blocks).max(-1, keepdims=True)
    byte = np.maximum(np.where(amax > 0, np.frexp(amax)[1] - 1 + 127, 0) - down, 1)
    scale = np.exp2(byte - 127.0)
    codes = (blocks / scale).astype(np.float32).astype(dtype).astype(np.float64)
    return np.moveaxis((codes * scale).reshape(v.shape), -1, axis)


WIDE = False


def mx_kscale(k):
    if not WIDE:
        return np.ones(k)
    levels = np.array([10, -10, 5, -5, 0])
    if k % 512:
        return np.exp2(np.random.permutation(np.resize(levels, k // 32))).repeat(32)
    a = np.empty((k // 512, 16))
    for p in range(k // 512):
        a[p, :8] = np.random.permutation(np.resize(levels, 8))
        for g in range(8):
            far = levels[np.abs(levels - a[p, g]) >= 10]
            a[p, g + 8] = far[np.random.randint(len(far))]
    return np.exp2(a.ravel()).repeat(32)


def f64(x):
    return np.asarray(x).astype(np.float64)


def striped(idx):
    return np.tile(np.asarray(idx).reshape(-1, 16).T, (8, 1)).astype(np.uint16)


def unstriped(offs):
    return offs[:16].T.reshape(-1).astype(np.int64)


E2M1 = np.array([0.0, 0.5, 1.0, 1.5, 2.0, 3.0, 4.0, 6.0, -0.0, -0.5, -1.0, -1.5, -2.0, -3.0, -4.0, -6.0])


def pack_weight(w, fmt):
    k, n = w.shape
    w = f64(np.asarray(w, np.float32).astype(ml_dtypes.bfloat16)).reshape(k // 32, 32, n)
    amax = np.abs(w).max(1)
    if fmt == "e4m3":
        byte = np.frexp(amax)[1] - 1 + 127 - 7
    else:
        mant, ex = np.frexp(amax / 6.0)
        byte = np.where(mant > 0.5, ex, ex - 1) + 127
    byte = np.clip(np.where(amax > 0, byte, 1), 1, 254)
    scaled = (w * np.exp2(127.0 - byte)[:, None, :]).reshape(k, n).astype(np.float32)
    by_word = np.ascontiguousarray(scaled.reshape(k // 512, 128, 4, n).transpose(0, 1, 3, 2))
    if fmt == "e4m3":
        words = by_word.astype(ml_dtypes.float8_e4m3fn).view(np.uint8)
    else:
        c = by_word.astype(ml_dtypes.float4_e2m1fn).view(np.uint8) & 0xF
        words = (c[..., 0::2] | (c[..., 1::2] << 4)).reshape(k // 512, 128, 2 * n)
    return np.ascontiguousarray(words), np.ascontiguousarray(byte.astype(np.uint8).reshape(k // 512, 16, n))


def unpack_weight(words, scales, fmt):
    g, _, n = scales.shape
    words = np.ascontiguousarray(words).reshape(g, 128, n, -1)
    if fmt == "e4m3":
        vals = words.view(ml_dtypes.float8_e4m3fn).astype(np.float64)
    else:
        nib = np.empty((g, 128, n, 4), np.uint8)
        nib[..., 0::2] = words & 0xF
        nib[..., 1::2] = words >> 4
        vals = E2M1[nib]
    vals = vals * np.repeat(np.exp2(scales.astype(np.float64) - 127.0), 8, axis=1)[..., None]
    return vals.transpose(0, 1, 3, 2).reshape(g * 512, n)


D, E, T, I, G, U, Q = 512, 512, 4096, 1024, 64, 512, 128


def setup_inputs():
    n = np.random.standard_normal
    idx = np.random.permutation(T)[:I]
    idx2 = np.random.permutation(U)[:G]
    fd = mx_kscale(D)
    fe = mx_kscale(E)
    keysp = pack_weight(n((D, T)) / fd[:, None], "e2m1")
    valsp = pack_weight(n((E, T)) / fe[:, None], "e2m1")
    return {
        "query": (n((D, Q)) * 0.6 / np.sqrt(D) * fd[:, None]).astype(np.float32),
        "keys_words": keysp[0],
        "keys_scales": keysp[1],
        "ptab": (0.5 * n((Q, U)) - 0.4).astype(np.float32),
        "age": (np.random.uniform(0.0, 2.0, (1, I))).astype(np.float32),
        "gout": (n((E, Q)) * 1 / np.sqrt(E) * fe[:, None]).astype(np.float32),
        "vals_words": valsp[0],
        "vals_scales": valsp[1],
        "old": (0.5 * n((Q, U))).astype(np.float32),
        "offs": striped(idx),
        "offs2": striped(idx2),
    }


def reference(query, keys_words, keys_scales, ptab, age, gout, vals_words, vals_scales, old, offs, offs2):
    idx = unstriped(offs)
    idx2 = unstriped(offs2)
    keysu = unpack_weight(keys_words, keys_scales, "e2m1")
    valsu = unpack_weight(vals_words, vals_scales, "e2m1")
    queryq = mxq(f64(query), 0, "e4m3")
    keysidxg = keysu[:, idx]
    a = queryq.T @ keysidxg
    tp = np.exp(f64(ptab)[:, idx2])
    tr1 = np.repeat(tp, I // G, axis=1)
    p = np.exp(a - f64(age) * tr1)
    z = np.sum(p, axis=1, keepdims=True)
    goutq = mxq(f64(gout), 0, "e4m3")
    valsidxg = valsu[:, idx]
    c0 = goutq.T @ valsidxg
    dz = np.sum(p * c0, axis=1, keepdims=True) / np.square(z) * (-1.0)
    dp = 1.0 / z * c0 + dz
    dtr1 = dp * p * (-1.0) * f64(age)
    dtp = dtr1.reshape(Q, G, I // G).sum(axis=2)
    gs = dtp * tp * 64.0
    gf = np.zeros((Q, U))
    gf[:, idx2] = gs
    y = f64(old) + gf
    return y

from contextlib import ExitStack

import concourse.mybir as mybir
from concourse.masks import make_identity

F32 = mybir.dt.float32
BF16 = mybir.dt.bfloat16
I32 = mybir.dt.int32
U32 = mybir.dt.uint32
U16 = mybir.dt.uint16
U8 = mybir.dt.uint8
FP8X4 = mybir.dt.float8_e4m3fn_x4
FP4X4 = mybir.dt.float4_e2m1fn_x4
ALU = mybir.AluOpType
ACT = mybir.ActivationFunctionType
AXIS = mybir.AxisListType

P = 128
PACK = 4
T = 4096
SLOTS = 1024
PAGES = 64
PAGE = 16
U = 512
Q = 128
HALF = 512
HALVES = SLOTS // HALF
TILES = HALF // P
SCALE_ROWS = 16
SCALE_AT = P - SCALE_ROWS
AGE_ROWS = SLOTS // P
AGE_AT = P - AGE_ROWS
GAIN = -64.0

FLOPS = 2 * 2 * 512 * Q * SLOTS


def tile_attend_bpagerate_kernel(tc, query, keys_words, keys_scales, ptab, age, gout, vals_words, vals_scales, old, offs, offs2, out):
    nc = tc.nc
    with ExitStack() as ctx:
        lists = ctx.enter_context(tc.tile_pool(name="lists", bufs=1))
        sb = ctx.enter_context(tc.tile_pool(name="sb", bufs=1))
        ps = ctx.enter_context(tc.psum_pool(name="ps", bufs=1))

        slot_list = lists.tile([P, SLOTS // 16], U16, name="slot_list")
        page_list = lists.tile([P, PAGES // 16], U16, name="page_list")

        ks_win = sb.tile([P, T], U8, name="ks_win", tag="ks_then_vw", align_bytes=64)
        vs_win = sb.tile([P, T], U8, name="vs_win", align_bytes=64)
        kw_win = sb.tile([P, T], U16, name="kw_win", align_bytes=64)
        ptab_win = sb.tile([P, U], F32, name="ptab_win", align_bytes=64)
        q_raw = sb.tile([P, PACK, Q], F32, name="q_raw", align_bytes=64)
        g_raw = sb.tile([P, PACK, Q], F32, name="g_raw", tag="g_then_old", align_bytes=64)
        age_rows = sb.tile([P, P], F32, name="age_rows", align_bytes=64)

        nc.scalar.dma_start(ptab_win[:], ptab)
        nc.sync.dma_start(page_list[:], offs2)
        nc.sync.dma_start(slot_list[:], offs)
        nc.sync.dma_start(ks_win[SCALE_AT:P, :].bitcast(I32), keys_scales[0].bitcast(I32))
        nc.sync.dma_start(age_rows[AGE_AT:P, :], age.rearrange("o (t p) -> (o t) p", p=P))
        nc.sync.dma_start(q_raw[:], query.rearrange("(p j) w -> p j w", j=PACK))
        nc.sync.dma_start(kw_win[:].bitcast(I32), keys_words[0].bitcast(I32))
        nc.sync.dma_start(vs_win[SCALE_AT:P, :].bitcast(I32), vals_scales[0].bitcast(I32))
        nc.sync.dma_start(g_raw[:], gout.rearrange("(p j) w -> p j w", j=PACK))

        nc.vector.memset(ks_win[0:SCALE_AT, :].bitcast(I32), 0)
        nc.vector.memset(vs_win[0:SCALE_AT, :].bitcast(I32), 0)
        nc.vector.memset(age_rows[0:AGE_AT, :], 0.0)

        warm = sb.tile([P, 1], F32, name="warm")
        nc.gpsimd.memset(warm[:], 0.0)
        warm_out = sb.tile([P, 1], F32, name="warm_out")
        nc.scalar.activation(warm_out[:], warm[:], ACT.Exp)

        ident = sb.tile([P, P], F32, name="ident", align_bytes=64)
        make_identity(nc, ident[:])
        k_plane = sb.tile([P, SLOTS], U8, name="k_plane", align_bytes=64)
        v_plane = sb.tile([P, SLOTS], U8, name="v_plane", align_bytes=64)
        placed = sb.tile([P, U], F32, name="placed", align_bytes=64)
        nc.gpsimd.memset(k_plane[:].bitcast(I32), 0)
        nc.gpsimd.memset(v_plane[:].bitcast(I32), 0)
        nc.gpsimd.memset(placed[:], 0.0)

        def move_scales(queue, plane, picked):
            for quad in range(4):
                queue.dma_start(
                    plane[32 * quad : 32 * quad + 4, :].bitcast(I32),
                    picked[SCALE_AT + 4 * quad : SCALE_AT + 4 * quad + 4, :].bitcast(I32),
                )

        def interleave(name, raw, tag):
            grouped = sb.tile([P, Q, PACK], BF16, name=name, tag=tag, align_bytes=64)
            nc.scalar.copy(grouped[:], raw[:].rearrange("p j w -> p w j"))
            return grouped

        def quantize(name, grouped):
            codes = sb.tile([P, Q], U32, name=name + "_codes", align_bytes=64)
            scales = sb.tile([P, Q], U8, name=name + "_scales", align_bytes=64)
            nc.vector.quantize_mx(out=codes[:].bitcast(FP8X4), scales=scales[:], in_=grouped[:].rearrange("p w j -> p (w j)"))
            return codes, scales

        def half_list(h):
            return slot_list[:, h * HALF // 16 : (h + 1) * HALF // 16]

        log_rate = sb.tile([P, PAGES], F32, name="log_rate")
        nc.vector.tensor_copy(log_rate[:], ptab_win[:].indirect(page_list[:]))
        ks_picked = sb.tile([P, SLOTS], U8, name="ks_picked", align_bytes=64)
        nc.vector.tensor_copy(ks_picked[:], ks_win[:].indirect(slot_list[:]))
        move_scales(nc.sync, k_plane, ks_picked)
        vw_win = sb.tile([P, T], U16, name="vw_win", tag="ks_then_vw", align_bytes=64)
        nc.sync.dma_start(vw_win[:].bitcast(I32), vals_words[0].bitcast(I32))

        q_grouped = interleave("q_grouped", q_raw, "q_grouped")

        age_bank = ps.tile([P, HALF], F32, name="age_bank", tag="bank0")
        nc.tensor.transpose(age_bank[:, 0:P], age_rows[:], ident[:])
        age_col = sb.tile([P, AGE_ROWS], F32, name="age_col", tag="age_then_g", align_bytes=64)
        nc.scalar.copy(age_col[:], age_bank[:, AGE_AT:P])

        q_codes, q_scales = quantize("q", q_grouped)
        rate = sb.tile([P, PAGES, PAGE], F32, name="rate", align_bytes=64)
        for h in range(HALVES):
            pages = slice(h * PAGES // HALVES, (h + 1) * PAGES // HALVES)
            nc.scalar.activation(rate[:, pages, :], log_rate[:, pages].unsqueeze(2).to_broadcast([P, PAGES // HALVES, PAGE]), ACT.Exp)
        rate_flat = rate[:].rearrange("p g j -> p (g j)")

        age_wide = []
        for h in range(HALVES):
            bank = ps.tile([P, HALF], F32, name=f"age_wide{h}", tag=f"bank{2 + h}")
            for t in range(TILES):
                col = h * TILES + t
                nc.tensor.transpose(bank[:, t * P : (t + 1) * P], age_col[:, col : col + 1].to_broadcast([P, P]), ident[:])
            age_wide.append(bank)

        fade_t = sb.tile([P, SLOTS], F32, name="fade_t", align_bytes=64)
        neg_logit = []
        for h in range(HALVES):
            rate_t = ps.tile([P, HALF], F32, name=f"rate_t{h}", tag=f"bank{4 + h}")
            for t in range(TILES):
                cols = slice(h * HALF + t * P, h * HALF + (t + 1) * P)
                nc.tensor.transpose(rate_t[:, t * P : (t + 1) * P], rate_flat[:, cols], ident[:])
            for t in range(TILES):
                col = h * TILES + t
                nc.scalar.activation(fade_t[:, col * P : (col + 1) * P], rate_t[:, t * P : (t + 1) * P], ACT.Copy, scale=age_col[:, col : col + 1])
            bank = ps.tile([P, HALF], F32, name=f"neg_logit{h}", tag=f"bank{6 + h}")
            for t in range(TILES):
                col = h * TILES + t
                nc.tensor.matmul(bank[:, t * P : (t + 1) * P], lhsT=fade_t[:, col * P : (col + 1) * P], rhs=ident[:], start=(t == 0), stop=False, is_transpose=True)
            neg_logit.append(bank)

        g_grouped = interleave("g_grouped", g_raw, "age_then_g")

        weight = sb.tile([P, SLOTS], F32, name="weight", align_bytes=64)
        z_parts = sb.tile([P, HALVES], F32, name="z_parts")
        for h in range(HALVES):
            k_picked = sb.tile([P, HALF], U16, name=f"k_picked{h}", align_bytes=64)
            nc.vector.tensor_copy(k_picked[:], kw_win[:].indirect(half_list(h)))
            score_t = ps.tile([P, HALF], F32, name=f"score_t{h}", tag=f"bank{5 - h}")
            for t in range(TILES):
                nc.tensor.matmul_mx(
                    out=score_t[:, t * P : (t + 1) * P],
                    lhsT=k_picked[:, t * P : (t + 1) * P].bitcast(FP4X4),
                    lhsT_scale=k_plane[:, h * HALF + t * P : h * HALF + (t + 1) * P],
                    rhs=q_codes[:].bitcast(FP8X4),
                    rhs_scale=q_scales[:],
                    start=True,
                    stop=True,
                )
            neg_score_t = sb.tile([P, HALF], F32, name=f"neg_score_t{h}", align_bytes=64)
            nc.scalar.activation(neg_score_t[:], score_t[:], ACT.Copy, scale=-1.0)
            for t in range(TILES):
                nc.tensor.matmul(neg_logit[h][:, t * P : (t + 1) * P], lhsT=neg_score_t[:, t * P : (t + 1) * P], rhs=ident[:], start=False, stop=(t == TILES - 1), is_transpose=True)
            nc.scalar.activation(weight[:, h * HALF : (h + 1) * HALF], neg_logit[h][:], ACT.Exp, scale=-1.0, accum_out=z_parts[:, h : h + 1])

        vs_picked = sb.tile([P, SLOTS], U8, name="vs_picked", align_bytes=64)
        nc.vector.tensor_copy(vs_picked[:], vs_win[:].indirect(slot_list[:]))

        move_scales(nc.sync, v_plane, vs_picked)
        old_sb = sb.tile([P, U], F32, name="old_sb", tag="g_then_old", align_bytes=64)
        nc.sync.dma_start(old_sb[:], old)

        g_codes, g_scales = quantize("g", g_grouped)

        value_dot = []
        for h in range(HALVES):
            v_picked = sb.tile([P, HALF], U16, name=f"v_picked{h}", align_bytes=64)
            nc.vector.tensor_copy(v_picked[:], vw_win[:].indirect(half_list(h)))
            bank = ps.tile([P, HALF], F32, name=f"value_dot{h}", tag=f"bank{h}")
            nc.tensor.matmul_mx(
                out=bank[:],
                lhsT=g_codes[:].bitcast(FP8X4),
                lhsT_scale=g_scales[:],
                rhs=v_picked[:].bitcast(FP4X4),
                rhs_scale=v_plane[:, h * HALF : (h + 1) * HALF],
                start=True,
                stop=True,
            )
            value_dot.append(bank)

        aged = sb.tile([P, SLOTS], F32, name="aged", align_bytes=64)
        scratch = sb.tile([P, SLOTS], F32, name="scratch", align_bytes=64)
        s_parts = sb.tile([P, HALVES], F32, name="s_parts")
        cols = [slice(h * HALF, (h + 1) * HALF) for h in range(HALVES)]
        nc.vector.tensor_tensor(aged[:, cols[0]], weight[:, cols[0]], age_wide[0][:], ALU.mult)
        for h in range(HALVES):
            nc.vector.scalar_tensor_tensor(scratch[:, cols[h]], value_dot[h][:], 1.0, weight[:, cols[h]], ALU.mult, ALU.mult, accum_out=s_parts[:, h : h + 1])
        z = sb.tile([P, 1], F32, name="z")
        inv_z = sb.tile([P, 1], F32, name="inv_z")
        nc.vector.tensor_tensor(z[:], z_parts[:, 0:1], z_parts[:, 1:2], ALU.add)
        nc.vector.reciprocal(inv_z[:], z[:])
        nc.vector.tensor_tensor(aged[:, cols[1]], weight[:, cols[1]], age_wide[1][:], ALU.mult)
        mean_dot = sb.tile([P, 1], F32, name="mean_dot")
        nc.vector.tensor_scalar(mean_dot[:], s_parts[:, 0:1], s_parts[:, 1:2], inv_z[:], ALU.add, ALU.mult)
        page_gain = sb.tile([P, PAGES], F32, name="page_gain")
        page_rate = sb.tile([P, PAGES], F32, name="page_rate")
        nc.scalar.activation(page_rate[:], rate[:, :, 0], ACT.Copy, scale=GAIN)
        nc.scalar.activation(page_gain[:], page_rate[:], ACT.Copy, scale=inv_z[:])

        term = sb.tile([P, SLOTS], F32, name="term", align_bytes=64)
        page_sum = sb.tile([P, PAGES], F32, name="page_sum")
        for h in range(HALVES):
            nc.vector.scalar_tensor_tensor(term[:, cols[h]], value_dot[h][:], mean_dot[:], aged[:, cols[h]], ALU.subtract, ALU.mult)
        for h in range(HALVES):
            nc.vector.tensor_reduce(
                page_sum[:, h * PAGES // HALVES : (h + 1) * PAGES // HALVES],
                term[:, cols[h]].rearrange("p (g j) -> p g j", j=PAGE),
                AXIS.X,
                ALU.add,
            )
        nc.vector.tensor_tensor(placed[:].indirect(page_list[:]), page_sum[:], page_gain[:], ALU.mult)

        result = sb.tile([P, U], F32, name="result", align_bytes=64)
        for c, queue in enumerate((nc.sync, nc.scalar)):
            part = slice(c * U // 2, (c + 1) * U // 2)
            nc.vector.tensor_tensor(result[:, part], placed[:, part], old_sb[:, part], ALU.add)
            queue.dma_start(out[:, part], result[:, part])
